import numpy as np
import ml_dtypes


def mxq(x, axis, fmt="e4m3"):
    dtype, down = {"e4m3": (ml_dtypes.float8_e4m3fn, 7), "e5m2": (ml_dtypes.float8_e5m2, 14)}[fmt]
    v = np.moveaxis(np.asarray(x, np.float32).astype(ml_dtypes.bfloat16).astype(np.float64), axis, -1)
    blocks = v.reshape(v.shape[:-1] + (-1, 32))
    amax = np.abs(blocks).max(-1, keepdims=True)
    byte = np.maximum(np.where(amax > 0, np.frexp(amax)[1] - 1 + 127, 0) - down, 1)
    scale = np.exp2(byte - 127.0)
    codes = (blocks / scale).astype(np.float32).astype(dtype).astype(np.float64)
    return np.moveaxis((codes * scale).reshape(v.shape), -1, axis)


WIDE = False


def mx_kscale(k):
    if not WIDE:
        return np.ones(k)
    levels = np.array([30, -30])
    if k % 512:
        return np.exp2(np.random.permutation(np.resize(levels, k // 32))).repeat(32)
    a = np.empty((k // 512, 16))
    for p in range(k // 512):
        a[p, :8] = np.random.permutation(np.resize(levels, 8))
        for g in range(8):
            far = levels[np.abs(levels - a[p, g]) >= 10]
            a[p, g + 8] = far[np.random.randint(len(far))]
    return np.exp2(a.ravel()).repeat(32)


def f64(x):
    return np.asarray(x).astype(np.float64)


def striped(idx):
    return np.tile(idx.reshape(-1, 16).T, (8, 1)).astype(np.uint16)


def unstriped(offs):
    return offs[:16].T.reshape(-1).astype(np.int64)


E2M1 = np.array([0.0, 0.5, 1.0, 1.5, 2.0, 3.0, 4.0, 6.0, -0.0, -0.5, -1.0, -1.5, -2.0, -3.0, -4.0, -6.0])


def pack_weight(w, fmt):
    k, n = w.shape
    w = f64(np.asarray(w, np.float32).astype(ml_dtypes.bfloat16)).reshape(k // 32, 32, n)
    amax = np.abs(w).max(1)
    if fmt == "e4m3":
        byte = np.frexp(amax)[1] - 1 + 127 - 7
    else:
        mant, ex = np.frexp(amax / 6.0)
        byte = np.where(mant > 0.5, ex, ex - 1) + 127
    byte = np.clip(np.where(amax > 0, byte, 1), 1, 254)
    scaled = (w * np.exp2(127.0 - byte)[:, None, :]).reshape(k, n).astype(np.float32)
    by_word = np.ascontiguousarray(scaled.reshape(k // 512, 128, 4, n).transpose(0, 1, 3, 2))
    if fmt == "e4m3":
        words = by_word.astype(ml_dtypes.float8_e4m3fn).view(np.uint8)
    else:
        c = by_word.astype(ml_dtypes.float4_e2m1fn).view(np.uint8) & 0xF
        words = (c[..., 0::2] | (c[..., 1::2] << 4)).reshape(k // 512, 128, 2 * n)
    return np.ascontiguousarray(words), np.ascontiguousarray(byte.astype(np.uint8).reshape(k // 512, 16, n))


def unpack_weight(words, scales, fmt):
    g, _, n = scales.shape
    words = np.ascontiguousarray(words).reshape(g, 128, n, -1)
    if fmt == "e4m3":
        vals = words.view(ml_dtypes.float8_e4m3fn).astype(np.float64)
    else:
        nib = np.empty((g, 128, n, 4), np.uint8)
        nib[..., 0::2] = words & 0xF
        nib[..., 1::2] = words >> 4
        vals = E2M1[nib]
    vals = vals * np.repeat(np.exp2(scales.astype(np.float64) - 127.0), 8, axis=1)[..., None]
    return vals.transpose(0, 1, 3, 2).reshape(g * 512, n)


K, T, E, C, N = 256, 1024, 4, 512, 1536


def by_expert(wq, xq):
    return np.concatenate([wq[e].T @ xq[:, e * C:(e + 1) * C] for e in range(E)], axis=1)


def setup_inputs():
    n = np.random.standard_normal
    s = mx_kscale(N)[:, None]
    first = np.random.permutation(np.repeat(np.arange(E), T // E))
    second = (first + 1 + np.random.permutation(np.repeat(np.arange(E - 1), -(-T // (E - 1)))[:T])) % E
    while np.bincount(second, minlength=E).max() != T // E:
        load = np.bincount(second, minlength=E); hi, lo = int(load.argmax()), int(load.argmin())
        t = np.flatnonzero((second == hi) & (first != lo))[0]; second[t] = lo
    slot_token = np.empty(E * C, np.int64); pos = np.empty((2, T), np.int64); fill = np.zeros(E, np.int64)
    place = np.stack([np.random.permutation(C) for _ in range(E)])
    for r, deal in enumerate((first, second)):
        for t in np.random.permutation(T):
            e = deal[t]; j = e * C + place[e, fill[e]]; fill[e] += 1; slot_token[j] = t; pos[r, t] = j
    g = np.random.uniform(0.2, 0.8, T)
    w_slot = np.empty(E * C); w_slot[pos[0]] = g; w_slot[pos[1]] = 1.0 - g
    w = [pack_weight(m, "e2m1") for m in n((E + 1, N, K)) / np.sqrt(N) / s[None]]
    return {
        "dyT": (n((N, T)) * s).astype(np.float32),
        "w_words": np.stack([m[0] for m in w]),
        "w_scales": np.stack([m[1] for m in w]),
        "gate": np.tile(w_slot, (N, 1)).astype(np.float32),
        "offs": striped(slot_token),
        "pos1": striped(pos[0]),
        "pos2": striped(pos[1]),
    }


def reference(dyT, w_words, w_scales, gate, offs, pos1, pos2):
    idx = unstriped(offs)
    w = np.stack([unpack_weight(w_words[e], w_scales[e], "e2m1") for e in range(E + 1)])
    gq = mxq(f64(gate) * f64(dyT)[:, idx], 0, "e5m2")
    wq = w
    ds = wq[E].T @ mxq(f64(dyT), 0, "e5m2")
    dx = by_expert(wq, gq)
    return ds + dx[:, unstriped(pos1)] + dx[:, unstriped(pos2)]

@@ -1,0 +1,199 @@
+from contextlib import ExitStack
+
+import concourse.mybir as mybir
+
+K, T, E, C, N = 256, 1024, 4, 512, 1536
+S = E * C
+FLOPS = 2 * N * K * (S + T)
+BYTES = 4 * N * T + (E + 1) * N * K // 2 + (E + 1) * N * K // 32 + 4 * S + 2 * 128 * (S + 2 * T) // 16 + 4 * K * T
+
+F32 = mybir.dt.float32
+BF16 = mybir.dt.bfloat16
+I32 = mybir.dt.int32
+U32 = mybir.dt.uint32
+U16 = mybir.dt.uint16
+U8 = mybir.dt.uint8
+E5M2 = mybir.dt.float8_e5m2_x4
+E2M1 = mybir.dt.float4_e2m1fn_x4
+MULT = mybir.AluOpType.mult
+ADD = mybir.AluOpType.add
+
+P = 128
+PACK = 4
+PASSES = N // (P * PACK)
+W = 512
+KB = K // P
+HALVES = T // W
+
+
+def tile_moe_bds_lin_none_kernel(tc, dyT, w_words, w_scales, gate, offs, pos1, pos2, out):
+    nc = tc.nc
+    with ExitStack() as ctx:
+        held = ctx.enter_context(tc.tile_pool(name="held", bufs=1))
+        ring = ctx.enter_context(tc.tile_pool(name="ring", bufs=3))
+        psum = ctx.enter_context(tc.psum_pool(name="psum", bufs=1))
+
+        offs_sb = held.tile([P, S // 16], U16, name="offs_sb")
+        pos1_sb = held.tile([P, T // 16], U16, name="pos1_sb")
+        pos2_sb = held.tile([P, T // 16], U16, name="pos2_sb")
+        planes = [[held.tile([P, T], F32, name="plane%d_%d" % (a, t)) for t in range(PACK)] for a in range(PASSES)]
+        gates = [held.tile([P, C], F32, name="gate%d" % e) for e in range(E)]
+        words = [held.tile([P, PASSES * 2 * K], U8, name="words%d" % e, align_bytes=64) for e in range(E + 1)]
+        wscale = held.tile([P, (E + 1) * PASSES * K], U8, name="wscale", align_bytes=64)
+        raws = [[held.tile([P, PACK, W], F32, name="raw%d_%d" % (h, a)) for a in range(PASSES)] for h in range(HALVES)]
+        dx = [held.tile([P, S], F32, name="dx%d" % kb) for kb in range(KB)]
+        ds = [[held.tile([P, W], F32, name="ds%d_%d" % (kb, h)) for h in range(HALVES)] for kb in range(KB)]
+
+        dy_planes = dyT.rearrange("(a p t) c -> a t p c", p=P, t=PACK)
+        dy_rows = dyT.rearrange("(a p t) c -> a p t c", p=P, t=PACK)
+
+        def load_planes(a, ts):
+            for t in ts:
+                nc.sync.dma_start(out=planes[a][t][:], in_=dy_planes[a, t])
+
+        def load_gate(queue, e):
+            queue.dma_start(out=gates[e][:], in_=gate[0:P, e * C:(e + 1) * C])
+
+        def load_words(e):
+            nc.sync.dma_start(
+                out=words[e][:].bitcast(I32).rearrange("p (a k) -> p a k", a=PASSES),
+                in_=w_words[e].bitcast(I32).rearrange("a p k -> p a k"),
+            )
+
+        def load_raw(h, a):
+            nc.sync.dma_start(out=raws[h][a][:], in_=dy_rows[a][:, :, h * W:(h + 1) * W])
+
+        nc.gpsimd.memset(wscale[:].bitcast(I32), 0)
+        nc.sync.dma_start(offs_sb[:], offs)
+        load_gate(nc.scalar, 0)
+        load_planes(0, range(PACK))
+        load_gate(nc.sync, 1)
+        load_planes(1, range(PACK))
+        scale_rows = w_scales.bitcast(I32).rearrange("e a (q r) k -> r q (e a) k", r=4)
+        for r in range(4):
+            nc.sync.dma_start(
+                out=wscale[r:P:32, :].bitcast(I32).rearrange("q (g k) -> q g k", g=(E + 1) * PASSES),
+                in_=scale_rows[r],
+            )
+        load_words(0)
+        load_words(1)
+        load_words(E)
+        load_raw(0, 0)
+        load_planes(2, range(PACK))
+        load_raw(0, 1)
+        load_raw(0, 2)
+        load_gate(nc.sync, 2)
+        load_gate(nc.sync, 3)
+        load_words(2)
+        load_words(3)
+        for a in range(PASSES):
+            load_raw(1, a)
+        nc.sync.dma_start(pos1_sb[:], pos1)
+        nc.sync.dma_start(pos2_sb[:], pos2)
+
+        def weave(dst, src):
+            nc.scalar.copy(out=dst.rearrange("p (c t) -> p c t", t=PACK), in_=src.rearrange("p t c -> p c t"))
+
+        def quantize(codes, scales, woven):
+            nc.vector.quantize_mx(out=codes.bitcast(E5M2), scales=scales, in_=woven)
+
+        def multiply(banks, e, a, codes, scales):
+            for kb in range(KB):
+                w0 = a * 2 * K + kb * 2 * P
+                s0 = (e * PASSES + a) * K + kb * P
+                nc.tensor.matmul_mx(
+                    out=banks[kb][:],
+                    lhsT=words[e][:, w0:w0 + 2 * P].bitcast(E2M1),
+                    lhsT_scale=wscale[:, s0:s0 + P],
+                    rhs=codes.bitcast(E5M2),
+                    rhs_scale=scales,
+                    start=(a == 0),
+                    stop=(a == PASSES - 1),
+                )
+
+        units = [(0, 0), (1, 0), (0, 1), (1, 1), (0, 2), (1, 2)] + [(e, a) for e in (2, 3) for a in range(PASSES)]
+        shared_after = {1: (0, 0), 3: (0, 1), 4: (0, 2), 6: (1, 0), 7: (1, 1), 8: (1, 2)}
+        last = len(units) - 1
+        banks = {}
+        late_woven = []
+
+        def gather(u, c0, c1):
+            e, a = units[u]
+            g = ring.tile([P, PACK, c1 - c0], F32, name="g", tag="g")
+            for t in range(PACK):
+                nc.vector.tensor_tensor(
+                    g[:, t, :],
+                    planes[a][t][:].indirect(offs_sb[:, (e * C + c0) // 16:(e * C + c1) // 16]),
+                    gates[e][:, c0:c1],
+                    MULT,
+                )
+            return g
+
+        def bank_pair(key, slot):
+            if key not in banks:
+                banks[key] = [psum.tile([P, W], F32, name="bank", tag="bank%d_%d" % (slot, kb)) for kb in range(KB)]
+            return banks[key]
+
+        def finish_expert(u, codes, scales):
+            e, a = units[u]
+            multiply(bank_pair(e, e % 2), e, a, codes, scales)
+            if a == PASSES - 1:
+                for kb in range(KB):
+                    nc.scalar.copy(out=dx[kb][:, e * C:(e + 1) * C], in_=banks[e][kb][:])
+
+        def finish_shared(h, a, codes, scales):
+            multiply(bank_pair(E + h, 2 + h), E, a, codes, scales)
+            if a == PASSES - 1:
+                for kb in range(KB):
+                    nc.scalar.copy(out=ds[kb][h][:], in_=banks[E + h][kb][:])
+
+        def mx_tiles():
+            codes = ring.tile([P, W], U32, name="codes", tag="codes", align_bytes=64)
+            scales = ring.tile([P, W], U8, name="scales", tag="scales", align_bytes=64)
+            return codes, scales
+
+        for u in range(last):
+            g = gather(u, 0, C)
+            woven = ring.tile([P, PACK * W], BF16, name="woven", tag="woven", align_bytes=64)
+            weave(woven[:], g[:])
+            codes, scales = mx_tiles()
+            quantize(codes[:], scales[:], woven[:])
+            finish_expert(u, codes[:], scales[:])
+            if u in shared_after:
+                h, a = shared_after[u]
+                if h == 0:
+                    woven = ring.tile([P, PACK * W], BF16, name="woven", tag="woven", align_bytes=64)
+                    weave(woven[:], raws[h][a][:])
+                    codes, scales = mx_tiles()
+                    quantize(codes[:], scales[:], woven[:])
+                    finish_shared(h, a, codes[:], scales[:])
+                else:
+                    kept = held.tile([P, PACK * W], BF16, name="kept%d" % a, align_bytes=64)
+                    weave(kept[:], raws[h][a][:])
+                    late_woven.append(kept)
+
+        woven = held.tile([P, PACK * W], BF16, name="last_woven", tag="late", align_bytes=64)
+        codes, scales = mx_tiles()
+        half = C // 2
+        for c0 in (0, half):
+            g = gather(last, c0, c0 + half)
+            weave(woven[:, PACK * c0:PACK * (c0 + half)], g[:])
+            quantize(codes[:, c0:c0 + half], scales[:, c0:c0 + half], woven[:, PACK * c0:PACK * (c0 + half)])
+        finish_expert(last, codes[:], scales[:])
+
+        late_codes = held.tile([P, PASSES * W], U32, name="late_codes", tag="late", align_bytes=64)
+        late_scales = held.tile([P, PASSES * W], U8, name="late_scales", align_bytes=64)
+        for a in range(PASSES):
+            cols = slice(a * W, (a + 1) * W)
+            quantize(late_codes[:, cols], late_scales[:, cols], late_woven[a][:])
+            finish_shared(1, a, late_codes[:, cols], late_scales[:, cols])
+
+        for h in range(HALVES):
+            lists = slice(h * W // 16, (h + 1) * W // 16)
+            parts = [held.tile([P, W], F32, name="part%d_%d" % (kb, h)) for kb in range(KB)]
+            for kb in range(KB):
+                nc.vector.tensor_tensor(parts[kb][:], dx[kb][:].indirect(pos1_sb[:, lists]), ds[kb][h][:], ADD)
+            for kb in range(KB):
+                res = held.tile([P, W], F32, name="res%d_%d" % (kb, h))
+                nc.vector.tensor_tensor(res[:], dx[kb][:].indirect(pos2_sb[:, lists]), parts[kb][:], ADD)
+                nc.sync.dma_start(out=out[kb * P:(kb + 1) * P, h * W:(h + 1) * W], in_=res[:])

@@ -26,6 +26,10 @@ KB = K // P
 HALVES = T // W
 
 
+SPARE = 16
+RUN = 4
+
+
 def tile_moe_bds_lin_none_kernel(tc, dyT, w_words, w_scales, gate, offs, pos1, pos2, out):
     nc = tc.nc
     with ExitStack() as ctx:
@@ -36,23 +40,27 @@ def tile_moe_bds_lin_none_kernel(tc, dyT, w_words, w_scales, gate, offs, pos1, p
         offs_sb = held.tile([P, S // 16], U16, name="offs_sb")
         pos1_sb = held.tile([P, T // 16], U16, name="pos1_sb")
         pos2_sb = held.tile([P, T // 16], U16, name="pos2_sb")
-        planes = [[held.tile([P, T], F32, name="plane%d_%d" % (a, t)) for t in range(PACK)] for a in range(PASSES)]
-        gates = [held.tile([P, C], F32, name="gate%d" % e) for e in range(E)]
+        planes = [
+            [held.tile([P, T + SPARE], F32, name="plane", tag="plane%d_%d" % (a, t)) for t in range(PACK)]
+            for a in range(PASSES)
+        ]
+        gate_sb = held.tile([P, S], F32, name="gate_sb")
         words = [held.tile([P, PASSES * 2 * K], U8, name="words%d" % e, align_bytes=64) for e in range(E + 1)]
         wscale = held.tile([P, (E + 1) * PASSES * K], U8, name="wscale", align_bytes=64)
-        raws = [[held.tile([P, PACK, W], F32, name="raw%d_%d" % (h, a)) for a in range(PASSES)] for h in range(HALVES)]
-        dx = [held.tile([P, S], F32, name="dx%d" % kb) for kb in range(KB)]
-        ds = [[held.tile([P, W], F32, name="ds%d_%d" % (kb, h)) for h in range(HALVES)] for kb in range(KB)]
+        raws = [
+            [held.tile([P, PACK, W], F32, name="raw", tag="raw%d_%d" % (h, a), align_bytes=64) for a in range(PASSES)]
+            for h in range(HALVES)
+        ]
 
         dy_planes = dyT.rearrange("(a p t) c -> a t p c", p=P, t=PACK)
         dy_rows = dyT.rearrange("(a p t) c -> a p t c", p=P, t=PACK)
 
         def load_planes(a, ts):
             for t in ts:
-                nc.sync.dma_start(out=planes[a][t][:], in_=dy_planes[a, t])
+                nc.sync.dma_start(out=planes[a][t][:, 0:T], in_=dy_planes[a, t])
 
-        def load_gate(queue, e):
-            queue.dma_start(out=gates[e][:], in_=gate[0:P, e * C:(e + 1) * C])
+        def load_gate(queue, c0, c1):
+            queue.dma_start(out=gate_sb[:, c0:c1], in_=gate[0:P, c0:c1])
 
         def load_words(e):
             nc.sync.dma_start(
@@ -63,12 +71,19 @@ def tile_moe_bds_lin_none_kernel(tc, dyT, w_words, w_scales, gate, offs, pos1, p
         def load_raw(h, a):
             nc.sync.dma_start(out=raws[h][a][:], in_=dy_rows[a][:, :, h * W:(h + 1) * W])
 
+        for a in range(PASSES):
+            for t in range(PACK):
+                nc.gpsimd.memset(planes[a][t][:, T:T + SPARE], 0.0)
         nc.gpsimd.memset(wscale[:].bitcast(I32), 0)
         nc.sync.dma_start(offs_sb[:], offs)
-        load_gate(nc.scalar, 0)
-        load_planes(0, range(PACK))
-        load_gate(nc.sync, 1)
+        load_gate(nc.scalar, 0, C)
+        load_planes(0, [0])
+        load_gate(nc.sync, C, 2 * C)
+        load_planes(0, [1, 2, 3])
+        load_raw(0, 0)
         load_planes(1, range(PACK))
+        load_planes(2, range(PACK))
+        load_gate(nc.sync, 2 * C, S)
         scale_rows = w_scales.bitcast(I32).rearrange("e a (q r) k -> r q (e a) k", r=4)
         for r in range(4):
             nc.sync.dma_start(
@@ -77,22 +92,20 @@ def tile_moe_bds_lin_none_kernel(tc, dyT, w_words, w_scales, gate, offs, pos1, p
             )
         load_words(0)
         load_words(1)
-        load_words(E)
-        load_raw(0, 0)
-        load_planes(2, range(PACK))
         load_raw(0, 1)
         load_raw(0, 2)
-        load_gate(nc.sync, 2)
-        load_gate(nc.sync, 3)
-        load_words(2)
-        load_words(3)
+        for e in (E, 2, 3):
+            load_words(e)
         for a in range(PASSES):
             load_raw(1, a)
         nc.sync.dma_start(pos1_sb[:], pos1)
         nc.sync.dma_start(pos2_sb[:], pos2)
 
         def weave(dst, src):
-            nc.scalar.copy(out=dst.rearrange("p (c t) -> p c t", t=PACK), in_=src.rearrange("p t c -> p c t"))
+            nc.scalar.copy(
+                out=dst.rearrange("p (c i t) -> p c t i", t=PACK, i=RUN),
+                in_=src.rearrange("p t (c i) -> p c t i", i=RUN),
+            )
 
         def quantize(codes, scales, woven):
             nc.vector.quantize_mx(out=codes.bitcast(E5M2), scales=scales, in_=woven)
@@ -111,89 +124,124 @@ def tile_moe_bds_lin_none_kernel(tc, dyT, w_words, w_scales, gate, offs, pos1, p
                     stop=(a == PASSES - 1),
                 )
 
-        units = [(0, 0), (1, 0), (0, 1), (1, 1), (0, 2), (1, 2)] + [(e, a) for e in (2, 3) for a in range(PASSES)]
-        shared_after = {1: (0, 0), 3: (0, 1), 4: (0, 2), 6: (1, 0), 7: (1, 1), 8: (1, 2)}
-        last = len(units) - 1
-        banks = {}
-        late_woven = []
+        def gather_plane(g, a, t, s0, c0, c1):
+            nc.vector.tensor_tensor(
+                g[:, t, c0 - s0:c1 - s0],
+                planes[a][t][:].indirect(offs_sb[:, c0 // 16:c1 // 16]),
+                gate_sb[:, c0:c1],
+                MULT,
+            )
 
-        def gather(u, c0, c1):
-            e, a = units[u]
-            g = ring.tile([P, PACK, c1 - c0], F32, name="g", tag="g")
+        def gathered_tile(width):
+            return ring.tile([P, PACK, width], F32, name="g", tag="g", bufs=2)
+
+        def gather(a, c0, c1):
+            g = gathered_tile(c1 - c0)
             for t in range(PACK):
-                nc.vector.tensor_tensor(
-                    g[:, t, :],
-                    planes[a][t][:].indirect(offs_sb[:, (e * C + c0) // 16:(e * C + c1) // 16]),
-                    gates[e][:, c0:c1],
-                    MULT,
-                )
+                if (a, t, c0) == (0, 0, 0):
+                    gather_plane(g, a, t, c0, c0, c0 + C)
+                    gather_plane(g, a, t, c0, c0 + C, c1)
+                else:
+                    gather_plane(g, a, t, c0, c0, c1)
             return g
 
-        def bank_pair(key, slot):
-            if key not in banks:
-                banks[key] = [psum.tile([P, W], F32, name="bank", tag="bank%d_%d" % (slot, kb)) for kb in range(KB)]
-            return banks[key]
-
-        def finish_expert(u, codes, scales):
-            e, a = units[u]
-            multiply(bank_pair(e, e % 2), e, a, codes, scales)
-            if a == PASSES - 1:
-                for kb in range(KB):
-                    nc.scalar.copy(out=dx[kb][:, e * C:(e + 1) * C], in_=banks[e][kb][:])
-
-        def finish_shared(h, a, codes, scales):
-            multiply(bank_pair(E + h, 2 + h), E, a, codes, scales)
-            if a == PASSES - 1:
-                for kb in range(KB):
-                    nc.scalar.copy(out=ds[kb][h][:], in_=banks[E + h][kb][:])
+        def bank_pair(slot):
+            return [psum.tile([P, W], F32, name="bank", tag="bank%d_%d" % (slot, kb)) for kb in range(KB)]
 
         def mx_tiles():
-            codes = ring.tile([P, W], U32, name="codes", tag="codes", align_bytes=64)
-            scales = ring.tile([P, W], U8, name="scales", tag="scales", align_bytes=64)
+            codes = ring.tile([P, W], U32, name="codes", tag="codes", bufs=4, align_bytes=64)
+            scales = ring.tile([P, W], U8, name="scales", tag="scales", bufs=4, align_bytes=64)
             return codes, scales
 
-        for u in range(last):
-            g = gather(u, 0, C)
-            woven = ring.tile([P, PACK * W], BF16, name="woven", tag="woven", align_bytes=64)
-            weave(woven[:], g[:])
+        def woven_tile(behind=None):
+            if behind is not None:
+                return held.tile([P, PACK * W], BF16, name="woven", tag="raw%d_%d" % behind, align_bytes=64)
+            return ring.tile([P, PACK * W], BF16, name="woven", tag="woven", align_bytes=64)
+
+        expert_banks = [bank_pair(e) for e in range(E)]
+
+        early_codes = held.tile([P, PASSES * W], U32, name="early_codes", align_bytes=64)
+        early_scales = held.tile([P, PASSES * W], U8, name="early_scales", align_bytes=64)
+        late_woven = [held.tile([P, PACK * W], BF16, name="late_woven%d" % a, align_bytes=64) for a in range(PASSES)]
+        dx = []
+        ds = {}
+
+        def weave_shared(h, a):
+            if h == 0:
+                woven = woven_tile()
+                weave(woven[:], raws[h][a][:])
+                quantize(early_codes[:, a * W:(a + 1) * W], early_scales[:, a * W:(a + 1) * W], woven[:])
+            else:
+                weave(late_woven[a][:], raws[h][a][:])
+
+        def finish_expert(e, a, codes, scales):
+            multiply(expert_banks[e], e, a, codes, scales)
+            if a == PASSES - 1:
+                for kb in range(KB):
+                    nc.scalar.copy(out=dx[kb][:, e * C:(e + 1) * C], in_=expert_banks[e][kb][:])
+
+        def expert_unit(g, s0, e, a, behind=None):
+            woven = woven_tile(behind)
+            weave(woven[:], g[:, :, e * C - s0:(e + 1) * C - s0])
             codes, scales = mx_tiles()
             quantize(codes[:], scales[:], woven[:])
-            finish_expert(u, codes[:], scales[:])
-            if u in shared_after:
-                h, a = shared_after[u]
-                if h == 0:
-                    woven = ring.tile([P, PACK * W], BF16, name="woven", tag="woven", align_bytes=64)
-                    weave(woven[:], raws[h][a][:])
-                    codes, scales = mx_tiles()
-                    quantize(codes[:], scales[:], woven[:])
-                    finish_shared(h, a, codes[:], scales[:])
-                else:
-                    kept = held.tile([P, PACK * W], BF16, name="kept%d" % a, align_bytes=64)
-                    weave(kept[:], raws[h][a][:])
-                    late_woven.append(kept)
+            finish_expert(e, a, codes[:], scales[:])
+
+        def copy_out_shared(h, banks):
+            for kb in range(KB):
+                ds[kb, h] = held.tile([P, W], F32, name="ds", tag="plane0_%d" % (2 * h + kb))
+                nc.scalar.copy(out=ds[kb, h][:], in_=banks[kb][:])
+
+        shared_before = [[(0, 0)], [], [(0, 1), (0, 2)], [(1, 0), (1, 1)], [(1, 2)]]
+        pairs = [(a, e0) for e0 in (0, 2) for a in range(PASSES)][:-1]
+        for u, (a, e0) in enumerate(pairs):
+            for h, b in shared_before[u]:
+                weave_shared(h, b)
+            if a == PASSES - 1:
+                dx.extend(
+                    held.tile([P, S], F32, name="dx", tag="raw0_%d" % kb, align_bytes=64) for kb in range(KB)
+                )
+            g = gather(a, e0 * C, (e0 + 2) * C)
+            expert_unit(g, e0 * C, e0, a, shared_before[u][-1] if shared_before[u] else None)
+            expert_unit(g, e0 * C, e0 + 1, a)
+            if a == PASSES - 1:
+                banks = bank_pair(0)
+                for b in range(PASSES):
+                    multiply(banks, E, b, early_codes[:, b * W:(b + 1) * W], early_scales[:, b * W:(b + 1) * W])
+                for kb in range(KB):
+                    ds[kb, 0] = held.tile([P, W], F32, name="ds_early%d" % kb)
+                    nc.scalar.copy(out=ds[kb, 0][:], in_=banks[kb][:])
+
+        a = PASSES - 1
+        g = gather(a, 2 * C, 3 * C)
+        expert_unit(g, 2 * C, 2, a)
 
         woven = held.tile([P, PACK * W], BF16, name="last_woven", tag="late", align_bytes=64)
         codes, scales = mx_tiles()
         half = C // 2
+        g = gathered_tile(C)
         for c0 in (0, half):
-            g = gather(last, c0, c0 + half)
-            weave(woven[:, PACK * c0:PACK * (c0 + half)], g[:])
+            for t in range(PACK):
+                gather_plane(g, a, t, 3 * C, 3 * C + c0, 3 * C + c0 + half)
+            weave(woven[:, PACK * c0:PACK * (c0 + half)], g[:, :, c0:c0 + half])
             quantize(codes[:, c0:c0 + half], scales[:, c0:c0 + half], woven[:, PACK * c0:PACK * (c0 + half)])
-        finish_expert(last, codes[:], scales[:])
+        finish_expert(3, a, codes[:], scales[:])
 
         late_codes = held.tile([P, PASSES * W], U32, name="late_codes", tag="late", align_bytes=64)
         late_scales = held.tile([P, PASSES * W], U8, name="late_scales", align_bytes=64)
-        for a in range(PASSES):
-            cols = slice(a * W, (a + 1) * W)
-            quantize(late_codes[:, cols], late_scales[:, cols], late_woven[a][:])
-            finish_shared(1, a, late_codes[:, cols], late_scales[:, cols])
+        banks = bank_pair(1)
+        for b in range(PASSES):
+            cols = slice(b * W, (b + 1) * W)
+            quantize(late_codes[:, cols], late_scales[:, cols], late_woven[b][:])
+            multiply(banks, E, b, late_codes[:, cols], late_scales[:, cols])
+        copy_out_shared(1, banks)
 
         for h in range(HALVES):
             lists = slice(h * W // 16, (h + 1) * W // 16)
-            parts = [held.tile([P, W], F32, name="part%d_%d" % (kb, h)) for kb in range(KB)]
+            parts = [held.tile([P, W], F32, name="part", tag="plane1_%d" % (2 * h + kb)) for kb in range(KB)]
             for kb in range(KB):
-                nc.vector.tensor_tensor(parts[kb][:], dx[kb][:].indirect(pos1_sb[:, lists]), ds[kb][h][:], ADD)
+                nc.vector.tensor_tensor(parts[kb][:], dx[kb][:].indirect(pos1_sb[:, lists]), ds[kb, h][:], ADD)
             for kb in range(KB):
-                res = held.tile([P, W], F32, name="res%d_%d" % (kb, h))
+                res = held.tile([P, W], F32, name="res", tag="plane2_%d" % (2 * h + kb))
                 nc.vector.tensor_tensor(res[:], dx[kb][:].indirect(pos2_sb[:, lists]), parts[kb][:], ADD)
                 nc.sync.dma_start(out=out[kb * P:(kb + 1) * P, h * W:(h + 1) * W], in_=res[:])

@@ -41,7 +41,7 @@ def tile_moe_bds_lin_none_kernel(tc, dyT, w_words, w_scales, gate, offs, pos1, p
         pos1_sb = held.tile([P, T // 16], U16, name="pos1_sb")
         pos2_sb = held.tile([P, T // 16], U16, name="pos2_sb")
         planes = [
-            [held.tile([P, T + SPARE], F32, name="plane", tag="plane%d_%d" % (a, t)) for t in range(PACK)]
+            [held.tile([P, T + SPARE], F32, name="plane", tag="plane%d_%d" % (a, t), align_bytes=64) for t in range(PACK)]
             for a in range(PASSES)
         ]
         gate_sb = held.tile([P, S], F32, name="gate_sb")
@@ -76,8 +76,9 @@ def tile_moe_bds_lin_none_kernel(tc, dyT, w_words, w_scales, gate, offs, pos1, p
                 nc.gpsimd.memset(planes[a][t][:, T:T + SPARE], 0.0)
         nc.gpsimd.memset(wscale[:].bitcast(I32), 0)
         nc.sync.dma_start(offs_sb[:], offs)
-        load_gate(nc.scalar, 0, C)
+        load_gate(nc.scalar, 0, C // 2)
         load_planes(0, [0])
+        load_gate(nc.sync, C // 2, C)
         load_gate(nc.sync, C, 2 * C)
         load_planes(0, [1, 2, 3])
         load_raw(0, 0)
@@ -139,7 +140,8 @@ def tile_moe_bds_lin_none_kernel(tc, dyT, w_words, w_scales, gate, offs, pos1, p
             g = gathered_tile(c1 - c0)
             for t in range(PACK):
                 if (a, t, c0) == (0, 0, 0):
-                    gather_plane(g, a, t, c0, c0, c0 + C)
+                    gather_plane(g, a, t, c0, c0, c0 + C // 2)
+                    gather_plane(g, a, t, c0, c0 + C // 2, c0 + C)
                     gather_plane(g, a, t, c0, c0 + C, c1)
                 else:
                     gather_plane(g, a, t, c0, c0, c1)
@@ -148,100 +150,116 @@ def tile_moe_bds_lin_none_kernel(tc, dyT, w_words, w_scales, gate, offs, pos1, p
         def bank_pair(slot):
             return [psum.tile([P, W], F32, name="bank", tag="bank%d_%d" % (slot, kb)) for kb in range(KB)]
 
-        def mx_tiles():
-            codes = ring.tile([P, W], U32, name="codes", tag="codes", bufs=4, align_bytes=64)
-            scales = ring.tile([P, W], U8, name="scales", tag="scales", bufs=4, align_bytes=64)
+        def mx_tiles(width):
+            codes = ring.tile([P, width], U32, name="codes", tag="codes", align_bytes=64)
+            scales = ring.tile([P, width], U8, name="scales", tag="scales", align_bytes=64)
             return codes, scales
 
-        def woven_tile(behind=None):
-            if behind is not None:
-                return held.tile([P, PACK * W], BF16, name="woven", tag="raw%d_%d" % behind, align_bytes=64)
-            return ring.tile([P, PACK * W], BF16, name="woven", tag="woven", align_bytes=64)
+        def woven_tile(width, tag):
+            return held.tile([P, PACK * width], BF16, name="woven", tag=tag, align_bytes=64)
+
+        def copy_out(dst, banks):
+            for kb in range(KB):
+                nc.scalar.copy(out=dst[kb], in_=banks[kb][:])
 
         expert_banks = [bank_pair(e) for e in range(E)]
-
         early_codes = held.tile([P, PASSES * W], U32, name="early_codes", align_bytes=64)
         early_scales = held.tile([P, PASSES * W], U8, name="early_scales", align_bytes=64)
-        late_woven = [held.tile([P, PACK * W], BF16, name="late_woven%d" % a, align_bytes=64) for a in range(PASSES)]
+        early_woven = held.tile([P, PASSES * PACK * W], BF16, name="early_woven", align_bytes=64)
+        late_woven = held.tile([P, PASSES * PACK * W], BF16, name="late_woven", align_bytes=64)
+        shared_woven = [early_woven, late_woven]
         dx = []
         ds = {}
 
-        def weave_shared(h, a):
-            if h == 0:
-                woven = woven_tile()
-                weave(woven[:], raws[h][a][:])
-                quantize(early_codes[:, a * W:(a + 1) * W], early_scales[:, a * W:(a + 1) * W], woven[:])
-            else:
-                weave(late_woven[a][:], raws[h][a][:])
+        def words_of(a0, a1):
+            return slice(a0 * W, a1 * W)
 
-        def finish_expert(e, a, codes, scales):
-            multiply(expert_banks[e], e, a, codes, scales)
-            if a == PASSES - 1:
-                for kb in range(KB):
-                    nc.scalar.copy(out=dx[kb][:, e * C:(e + 1) * C], in_=expert_banks[e][kb][:])
+        def values_of(a0, a1):
+            return slice(a0 * PACK * W, a1 * PACK * W)
 
-        def expert_unit(g, s0, e, a, behind=None):
-            woven = woven_tile(behind)
-            weave(woven[:], g[:, :, e * C - s0:(e + 1) * C - s0])
-            codes, scales = mx_tiles()
-            quantize(codes[:], scales[:], woven[:])
-            finish_expert(e, a, codes[:], scales[:])
-
-        def copy_out_shared(h, banks):
-            for kb in range(KB):
-                ds[kb, h] = held.tile([P, W], F32, name="ds", tag="plane0_%d" % (2 * h + kb))
-                nc.scalar.copy(out=ds[kb, h][:], in_=banks[kb][:])
-
-        shared_before = [[(0, 0)], [], [(0, 1), (0, 2)], [(1, 0), (1, 1)], [(1, 2)]]
+        shared_before = [[(0, 0)], [], [(0, 1), (0, 2), (1, 0)], [(1, 1), (1, 2)], []]
+        woven_tags = ["raw0_0", "woven", "raw1_0", "raw1_2", "raw1_1"]
         pairs = [(a, e0) for e0 in (0, 2) for a in range(PASSES)][:-1]
         for u, (a, e0) in enumerate(pairs):
             for h, b in shared_before[u]:
-                weave_shared(h, b)
-            if a == PASSES - 1:
+                weave(shared_woven[h][:, values_of(b, b + 1)], raws[h][b][:])
+            early = [b for h, b in shared_before[u] if h == 0]
+            if early:
+                b0, b1 = early[0], early[-1] + 1
+                quantize(
+                    early_codes[:, words_of(b0, b1)], early_scales[:, words_of(b0, b1)], early_woven[:, values_of(b0, b1)]
+                )
+            g = gather(a, e0 * C, (e0 + 2) * C)
+            woven = woven_tile(2 * C, woven_tags[u])
+            for i in range(2):
+                weave(woven[:, values_of(i, i + 1)], g[:, :, i * C:(i + 1) * C])
+            codes, scales = mx_tiles(2 * C)
+            quantize(codes[:], scales[:], woven[:])
+            for i in range(2):
+                multiply(expert_banks[e0 + i], e0 + i, a, codes[:, words_of(i, i + 1)], scales[:, words_of(i, i + 1)])
+            if u == PASSES:
                 dx.extend(
                     held.tile([P, S], F32, name="dx", tag="raw0_%d" % kb, align_bytes=64) for kb in range(KB)
                 )
-            g = gather(a, e0 * C, (e0 + 2) * C)
-            expert_unit(g, e0 * C, e0, a, shared_before[u][-1] if shared_before[u] else None)
-            expert_unit(g, e0 * C, e0 + 1, a)
-            if a == PASSES - 1:
+                for e in range(2):
+                    copy_out([dx[kb][:, e * C:(e + 1) * C] for kb in range(KB)], expert_banks[e])
+            if u == PASSES + 1:
                 banks = bank_pair(0)
                 for b in range(PASSES):
-                    multiply(banks, E, b, early_codes[:, b * W:(b + 1) * W], early_scales[:, b * W:(b + 1) * W])
+                    multiply(banks, E, b, early_codes[:, words_of(b, b + 1)], early_scales[:, words_of(b, b + 1)])
                 for kb in range(KB):
                     ds[kb, 0] = held.tile([P, W], F32, name="ds_early%d" % kb)
-                    nc.scalar.copy(out=ds[kb, 0][:], in_=banks[kb][:])
+                copy_out([ds[kb, 0][:] for kb in range(KB)], banks)
 
         a = PASSES - 1
         g = gather(a, 2 * C, 3 * C)
-        expert_unit(g, 2 * C, 2, a)
+        woven = woven_tile(C, "woven")
+        weave(woven[:], g[:])
+        codes, scales = mx_tiles(C)
+        quantize(codes[:], scales[:], woven[:])
+        multiply(expert_banks[2], 2, a, codes[:], scales[:])
 
-        woven = held.tile([P, PACK * W], BF16, name="last_woven", tag="late", align_bytes=64)
-        codes, scales = mx_tiles()
-        half = C // 2
+        woven = woven_tile(C, "late")
+        codes, scales = mx_tiles(C)
         g = gathered_tile(C)
-        for c0 in (0, half):
+        half, quarter = C // 2, C // 4
+        for c0, c1 in ((0, half), (half, half + quarter), (half + quarter, C)):
             for t in range(PACK):
-                gather_plane(g, a, t, 3 * C, 3 * C + c0, 3 * C + c0 + half)
-            weave(woven[:, PACK * c0:PACK * (c0 + half)], g[:, :, c0:c0 + half])
+                gather_plane(g, a, t, 3 * C, 3 * C + c0, 3 * C + c1)
+            weave(woven[:, PACK * c0:PACK * c1], g[:, :, c0:c1])
+        for c0 in (0, half):
             quantize(codes[:, c0:c0 + half], scales[:, c0:c0 + half], woven[:, PACK * c0:PACK * (c0 + half)])
-        finish_expert(3, a, codes[:], scales[:])
+        multiply(expert_banks[3], 3, a, codes[:], scales[:])
+        for kb in range(KB):
+            for e in (2, 3):
+                nc.scalar.copy(out=dx[kb][:, e * C:(e + 1) * C], in_=expert_banks[e][kb][:])
 
-        late_codes = held.tile([P, PASSES * W], U32, name="late_codes", tag="late", align_bytes=64)
         late_scales = held.tile([P, PASSES * W], U8, name="late_scales", align_bytes=64)
+        final_codes = held.tile([P, W], U32, name="final_codes", tag="plane2_2", align_bytes=64)
+        quantize(final_codes[:], late_scales[:, words_of(a, a + 1)], late_woven[:, values_of(a, a + 1)])
+        late_codes = held.tile([P, a * W], U32, name="late_codes", tag="late", align_bytes=64)
+        quantize(late_codes[:], late_scales[:, words_of(0, a)], late_woven[:, values_of(0, a)])
         banks = bank_pair(1)
-        for b in range(PASSES):
-            cols = slice(b * W, (b + 1) * W)
-            quantize(late_codes[:, cols], late_scales[:, cols], late_woven[b][:])
-            multiply(banks, E, b, late_codes[:, cols], late_scales[:, cols])
-        copy_out_shared(1, banks)
+        for b in range(a):
+            multiply(banks, E, b, late_codes[:, words_of(b, b + 1)], late_scales[:, words_of(b, b + 1)])
+        multiply(banks, E, a, final_codes[:], late_scales[:, words_of(a, a + 1)])
+        for kb in range(KB):
+            ds[kb, 1] = held.tile([P, W], F32, name="ds", tag="plane0_%d" % kb, align_bytes=64)
+        copy_out([ds[kb, 1][:] for kb in range(KB)], banks)
 
         for h in range(HALVES):
             lists = slice(h * W // 16, (h + 1) * W // 16)
-            parts = [held.tile([P, W], F32, name="part", tag="plane1_%d" % (2 * h + kb)) for kb in range(KB)]
+            parts = [
+                held.tile([P, W], F32, name="part", tag="plane1_%d" % (2 * h + kb), align_bytes=64) for kb in range(KB)
+            ]
             for kb in range(KB):
                 nc.vector.tensor_tensor(parts[kb][:], dx[kb][:].indirect(pos1_sb[:, lists]), ds[kb, h][:], ADD)
             for kb in range(KB):
-                res = held.tile([P, W], F32, name="res", tag="plane2_%d" % (2 * h + kb))
-                nc.vector.tensor_tensor(res[:], dx[kb][:].indirect(pos2_sb[:, lists]), parts[kb][:], ADD)
-                nc.sync.dma_start(out=out[kb * P:(kb + 1) * P, h * W:(h + 1) * W], in_=res[:])
+                res = held.tile([P, W], F32, name="res", tag="plane2_%d" % (2 * h + kb), align_bytes=64)
+                cuts = (0, W - quarter, W) if (h, kb) == (HALVES - 1, KB - 1) else (0, W)
+                for c0, c1 in zip(cuts, cuts[1:]):
+                    t0, t1 = h * W + c0, h * W + c1
+                    nc.vector.tensor_tensor(
+                        res[:, c0:c1], dx[kb][:].indirect(pos2_sb[:, t0 // 16:t1 // 16]), parts[kb][:, c0:c1], ADD
+                    )
+                    nc.sync.dma_start(out=out[kb * P:(kb + 1) * P, t0:t1], in_=res[:, c0:c1])

@@ -73,8 +73,8 @@ def tile_moe_bds_lin_none_kernel(tc, dyT, w_words, w_scales, gate, offs, pos1, p
 
         for a in range(PASSES):
             for t in range(PACK):
-                nc.gpsimd.memset(planes[a][t][:, T:T + SPARE], 0.0)
-        nc.gpsimd.memset(wscale[:].bitcast(I32), 0)
+                nc.vector.memset(planes[a][t][:, T:T + SPARE], 0.0)
+        nc.vector.memset(wscale[:].bitcast(I32), 0)
         nc.sync.dma_start(offs_sb[:], offs)
         load_gate(nc.scalar, 0, C // 2)
         load_planes(0, [0])
@@ -133,11 +133,8 @@ def tile_moe_bds_lin_none_kernel(tc, dyT, w_words, w_scales, gate, offs, pos1, p
                 MULT,
             )
 
-        def gathered_tile(width):
-            return ring.tile([P, PACK, width], F32, name="g", tag="g", bufs=2)
-
-        def gather(a, c0, c1):
-            g = gathered_tile(c1 - c0)
+        def gather(a, c0, c1, slot):
+            g = held.tile([P, PACK, c1 - c0], F32, name="g", tag="g%d" % slot, align_bytes=64)
             for t in range(PACK):
                 if (a, t, c0) == (0, 0, 0):
                     gather_plane(g, a, t, c0, c0, c0 + C // 2)
@@ -189,7 +186,7 @@ def tile_moe_bds_lin_none_kernel(tc, dyT, w_words, w_scales, gate, offs, pos1, p
                 quantize(
                     early_codes[:, words_of(b0, b1)], early_scales[:, words_of(b0, b1)], early_woven[:, values_of(b0, b1)]
                 )
-            g = gather(a, e0 * C, (e0 + 2) * C)
+            g = gather(a, e0 * C, (e0 + 2) * C, u % 2)
             woven = woven_tile(2 * C, woven_tags[u])
             for i in range(2):
                 weave(woven[:, values_of(i, i + 1)], g[:, :, i * C:(i + 1) * C])
@@ -212,21 +209,19 @@ def tile_moe_bds_lin_none_kernel(tc, dyT, w_words, w_scales, gate, offs, pos1, p
                 copy_out([ds[kb, 0][:] for kb in range(KB)], banks)
 
         a = PASSES - 1
-        g = gather(a, 2 * C, 3 * C)
+        half, quarter = C // 2, C // 4
+        g = gather(a, 2 * C, S - half, 1)
         woven = woven_tile(C, "woven")
-        weave(woven[:], g[:])
+        weave(woven[:], g[:, :, 0:C])
         codes, scales = mx_tiles(C)
         quantize(codes[:], scales[:], woven[:])
         multiply(expert_banks[2], 2, a, codes[:], scales[:])
 
         woven = woven_tile(C, "late")
         codes, scales = mx_tiles(C)
-        g = gathered_tile(C)
-        half, quarter = C // 2, C // 4
-        for c0, c1 in ((0, half), (half, half + quarter), (half + quarter, C)):
-            for t in range(PACK):
-                gather_plane(g, a, t, 3 * C, 3 * C + c0, 3 * C + c1)
-            weave(woven[:, PACK * c0:PACK * c1], g[:, :, c0:c1])
+        weave(woven[:, 0:PACK * half], g[:, :, C:C + half])
+        g = gather(a, S - half, S, 0)
+        weave(woven[:, PACK * half:PACK * C], g[:])
         for c0 in (0, half):
             quantize(codes[:, c0:c0 + half], scales[:, c0:c0 + half], woven[:, PACK * c0:PACK * (c0 + half)])
         multiply(expert_banks[3], 3, a, codes[:], scales[:])
@@ -237,7 +232,7 @@ def tile_moe_bds_lin_none_kernel(tc, dyT, w_words, w_scales, gate, offs, pos1, p
         late_scales = held.tile([P, PASSES * W], U8, name="late_scales", align_bytes=64)
         final_codes = held.tile([P, W], U32, name="final_codes", tag="plane2_2", align_bytes=64)
         quantize(final_codes[:], late_scales[:, words_of(a, a + 1)], late_woven[:, values_of(a, a + 1)])
-        late_codes = held.tile([P, a * W], U32, name="late_codes", tag="late", align_bytes=64)
+        late_codes = held.tile([P, a * W], U32, name="late_codes", tag="g0", align_bytes=64)
         quantize(late_codes[:], late_scales[:, words_of(0, a)], late_woven[:, values_of(0, a)])
         banks = bank_pair(1)
         for b in range(a):
@@ -262,4 +257,5 @@ def tile_moe_bds_lin_none_kernel(tc, dyT, w_words, w_scales, gate, offs, pos1, p
                     nc.vector.tensor_tensor(
                         res[:, c0:c1], dx[kb][:].indirect(pos2_sb[:, t0 // 16:t1 // 16]), parts[kb][:, c0:c1], ADD
                     )
-                    nc.sync.dma_start(out=out[kb * P:(kb + 1) * P, t0:t1], in_=res[:, c0:c1])
+                    queue = nc.scalar if (kb, t1) == (KB - 1, T) else nc.sync
+                    queue.dma_start(out=out[kb * P:(kb + 1) * P, t0:t1], in_=res[:, c0:c1])

from contextlib import ExitStack

import concourse.mybir as mybir

K, T, E, C, N = 256, 1024, 4, 512, 1536
S = E * C
FLOPS = 2 * N * K * (S + T)
BYTES = 4 * N * T + (E + 1) * N * K // 2 + (E + 1) * N * K // 32 + 4 * S + 2 * 128 * (S + 2 * T) // 16 + 4 * K * T

F32 = mybir.dt.float32
BF16 = mybir.dt.bfloat16
I32 = mybir.dt.int32
U32 = mybir.dt.uint32
U16 = mybir.dt.uint16
U8 = mybir.dt.uint8
E5M2 = mybir.dt.float8_e5m2_x4
E2M1 = mybir.dt.float4_e2m1fn_x4
MULT = mybir.AluOpType.mult
ADD = mybir.AluOpType.add

P = 128
PACK = 4
PASSES = N // (P * PACK)
W = 512
KB = K // P
HALVES = T // W


SPARE = 16
RUN = 4


def tile_moe_bds_lin_none_kernel(tc, dyT, w_words, w_scales, gate, offs, pos1, pos2, out):
    nc = tc.nc
    with ExitStack() as ctx:
        held = ctx.enter_context(tc.tile_pool(name="held", bufs=1))
        ring = ctx.enter_context(tc.tile_pool(name="ring", bufs=3))
        psum = ctx.enter_context(tc.psum_pool(name="psum", bufs=1))

        offs_sb = held.tile([P, S // 16], U16, name="offs_sb")
        pos1_sb = held.tile([P, T // 16], U16, name="pos1_sb")
        pos2_sb = held.tile([P, T // 16], U16, name="pos2_sb")
        planes = [
            [held.tile([P, T + SPARE], F32, name="plane", tag="plane%d_%d" % (a, t), align_bytes=64) for t in range(PACK)]
            for a in range(PASSES)
        ]
        gate_sb = held.tile([P, S], F32, name="gate_sb")
        words = [held.tile([P, PASSES * 2 * K], U8, name="words%d" % e, align_bytes=64) for e in range(E + 1)]
        wscale = held.tile([P, (E + 1) * PASSES * K], U8, name="wscale", align_bytes=64)
        raws = [
            [held.tile([P, PACK, W], F32, name="raw", tag="raw%d_%d" % (h, a), align_bytes=64) for a in range(PASSES)]
            for h in range(HALVES)
        ]

        dy_planes = dyT.rearrange("(a p t) c -> a t p c", p=P, t=PACK)
        dy_rows = dyT.rearrange("(a p t) c -> a p t c", p=P, t=PACK)

        def load_planes(a, ts):
            for t in ts:
                nc.sync.dma_start(out=planes[a][t][:, 0:T], in_=dy_planes[a, t])

        def load_gate(queue, c0, c1):
            queue.dma_start(out=gate_sb[:, c0:c1], in_=gate[0:P, c0:c1])

        def load_words(e):
            nc.sync.dma_start(
                out=words[e][:].bitcast(I32).rearrange("p (a k) -> p a k", a=PASSES),
                in_=w_words[e].bitcast(I32).rearrange("a p k -> p a k"),
            )

        def load_raw(h, a):
            nc.sync.dma_start(out=raws[h][a][:], in_=dy_rows[a][:, :, h * W:(h + 1) * W])

        for a in range(PASSES):
            for t in range(PACK):
                nc.vector.memset(planes[a][t][:, T:T + SPARE], 0.0)
        nc.vector.memset(wscale[:].bitcast(I32), 0)
        nc.sync.dma_start(offs_sb[:], offs)
        load_gate(nc.scalar, 0, C // 2)
        load_planes(0, [0])
        load_gate(nc.sync, C // 2, C)
        load_gate(nc.sync, C, 2 * C)
        load_planes(0, [1, 2, 3])
        load_raw(0, 0)
        load_planes(1, range(PACK))
        load_planes(2, range(PACK))
        load_gate(nc.sync, 2 * C, S)
        scale_rows = w_scales.bitcast(I32).rearrange("e a (q r) k -> r q (e a) k", r=4)
        for r in range(4):
            nc.sync.dma_start(
                out=wscale[r:P:32, :].bitcast(I32).rearrange("q (g k) -> q g k", g=(E + 1) * PASSES),
                in_=scale_rows[r],
            )
        load_words(0)
        load_words(1)
        load_raw(0, 1)
        load_raw(0, 2)
        for e in (E, 2, 3):
            load_words(e)
        for a in range(PASSES):
            load_raw(1, a)
        nc.sync.dma_start(pos1_sb[:], pos1)
        nc.sync.dma_start(pos2_sb[:], pos2)

        def weave(dst, src):
            nc.scalar.copy(
                out=dst.rearrange("p (c i t) -> p c t i", t=PACK, i=RUN),
                in_=src.rearrange("p t (c i) -> p c t i", i=RUN),
            )

        def quantize(codes, scales, woven):
            nc.vector.quantize_mx(out=codes.bitcast(E5M2), scales=scales, in_=woven)

        def multiply(banks, e, a, codes, scales):
            for kb in range(KB):
                w0 = a * 2 * K + kb * 2 * P
                s0 = (e * PASSES + a) * K + kb * P
                nc.tensor.matmul_mx(
                    out=banks[kb][:],
                    lhsT=words[e][:, w0:w0 + 2 * P].bitcast(E2M1),
                    lhsT_scale=wscale[:, s0:s0 + P],
                    rhs=codes.bitcast(E5M2),
                    rhs_scale=scales,
                    start=(a == 0),
                    stop=(a == PASSES - 1),
                )

        def gather_plane(g, a, t, s0, c0, c1):
            nc.vector.tensor_tensor(
                g[:, t, c0 - s0:c1 - s0],
                planes[a][t][:].indirect(offs_sb[:, c0 // 16:c1 // 16]),
                gate_sb[:, c0:c1],
                MULT,
            )

        def gather(a, c0, c1, slot):
            g = held.tile([P, PACK, c1 - c0], F32, name="g", tag="g%d" % slot, align_bytes=64)
            for t in range(PACK):
                if (a, t, c0) == (0, 0, 0):
                    gather_plane(g, a, t, c0, c0, c0 + C // 2)
                    gather_plane(g, a, t, c0, c0 + C // 2, c0 + C)
                    gather_plane(g, a, t, c0, c0 + C, c1)
                else:
                    gather_plane(g, a, t, c0, c0, c1)
            return g

        def bank_pair(slot):
            return [psum.tile([P, W], F32, name="bank", tag="bank%d_%d" % (slot, kb)) for kb in range(KB)]

        def mx_tiles(width):
            codes = ring.tile([P, width], U32, name="codes", tag="codes", align_bytes=64)
            scales = ring.tile([P, width], U8, name="scales", tag="scales", align_bytes=64)
            return codes, scales

        def woven_tile(width, tag):
            return held.tile([P, PACK * width], BF16, name="woven", tag=tag, align_bytes=64)

        def copy_out(dst, banks):
            for kb in range(KB):
                nc.scalar.copy(out=dst[kb], in_=banks[kb][:])

        expert_banks = [bank_pair(e) for e in range(E)]
        early_codes = held.tile([P, PASSES * W], U32, name="early_codes", align_bytes=64)
        early_scales = held.tile([P, PASSES * W], U8, name="early_scales", align_bytes=64)
        early_woven = held.tile([P, PASSES * PACK * W], BF16, name="early_woven", align_bytes=64)
        late_woven = held.tile([P, PASSES * PACK * W], BF16, name="late_woven", align_bytes=64)
        shared_woven = [early_woven, late_woven]
        dx = []
        ds = {}

        def words_of(a0, a1):
            return slice(a0 * W, a1 * W)

        def values_of(a0, a1):
            return slice(a0 * PACK * W, a1 * PACK * W)

        shared_before = [[(0, 0)], [], [(0, 1), (0, 2), (1, 0)], [(1, 1), (1, 2)], []]
        woven_tags = ["raw0_0", "woven", "raw1_0", "raw1_2", "raw1_1"]
        pairs = [(a, e0) for e0 in (0, 2) for a in range(PASSES)][:-1]
        for u, (a, e0) in enumerate(pairs):
            for h, b in shared_before[u]:
                weave(shared_woven[h][:, values_of(b, b + 1)], raws[h][b][:])
            early = [b for h, b in shared_before[u] if h == 0]
            if early:
                b0, b1 = early[0], early[-1] + 1
                quantize(
                    early_codes[:, words_of(b0, b1)], early_scales[:, words_of(b0, b1)], early_woven[:, values_of(b0, b1)]
                )
            g = gather(a, e0 * C, (e0 + 2) * C, u % 2)
            woven = woven_tile(2 * C, woven_tags[u])
            for i in range(2):
                weave(woven[:, values_of(i, i + 1)], g[:, :, i * C:(i + 1) * C])
            codes, scales = mx_tiles(2 * C)
            quantize(codes[:], scales[:], woven[:])
            for i in range(2):
                multiply(expert_banks[e0 + i], e0 + i, a, codes[:, words_of(i, i + 1)], scales[:, words_of(i, i + 1)])
            if u == PASSES:
                dx.extend(
                    held.tile([P, S], F32, name="dx", tag="raw0_%d" % kb, align_bytes=64) for kb in range(KB)
                )
                for e in range(2):
                    copy_out([dx[kb][:, e * C:(e + 1) * C] for kb in range(KB)], expert_banks[e])
            if u == PASSES + 1:
                banks = bank_pair(0)
                for b in range(PASSES):
                    multiply(banks, E, b, early_codes[:, words_of(b, b + 1)], early_scales[:, words_of(b, b + 1)])
                for kb in range(KB):
                    ds[kb, 0] = held.tile([P, W], F32, name="ds_early%d" % kb)
                copy_out([ds[kb, 0][:] for kb in range(KB)], banks)

        a = PASSES - 1
        half, quarter = C // 2, C // 4
        g = gather(a, 2 * C, S - half, 1)
        woven = woven_tile(C, "woven")
        weave(woven[:], g[:, :, 0:C])
        codes, scales = mx_tiles(C)
        quantize(codes[:], scales[:], woven[:])
        multiply(expert_banks[2], 2, a, codes[:], scales[:])

        woven = woven_tile(C, "late")
        codes, scales = mx_tiles(C)
        weave(woven[:, 0:PACK * half], g[:, :, C:C + half])
        g = gather(a, S - half, S, 0)
        weave(woven[:, PACK * half:PACK * C], g[:])
        for c0 in (0, half):
            quantize(codes[:, c0:c0 + half], scales[:, c0:c0 + half], woven[:, PACK * c0:PACK * (c0 + half)])
        multiply(expert_banks[3], 3, a, codes[:], scales[:])
        for kb in range(KB):
            for e in (2, 3):
                nc.scalar.copy(out=dx[kb][:, e * C:(e + 1) * C], in_=expert_banks[e][kb][:])

        late_scales = held.tile([P, PASSES * W], U8, name="late_scales", align_bytes=64)
        final_codes = held.tile([P, W], U32, name="final_codes", tag="plane2_2", align_bytes=64)
        quantize(final_codes[:], late_scales[:, words_of(a, a + 1)], late_woven[:, values_of(a, a + 1)])
        late_codes = held.tile([P, a * W], U32, name="late_codes", tag="g0", align_bytes=64)
        quantize(late_codes[:], late_scales[:, words_of(0, a)], late_woven[:, values_of(0, a)])
        banks = bank_pair(1)
        for b in range(a):
            multiply(banks, E, b, late_codes[:, words_of(b, b + 1)], late_scales[:, words_of(b, b + 1)])
        multiply(banks, E, a, final_codes[:], late_scales[:, words_of(a, a + 1)])
        for kb in range(KB):
            ds[kb, 1] = held.tile([P, W], F32, name="ds", tag="plane0_%d" % kb, align_bytes=64)
        copy_out([ds[kb, 1][:] for kb in range(KB)], banks)

        for h in range(HALVES):
            lists = slice(h * W // 16, (h + 1) * W // 16)
            parts = [
                held.tile([P, W], F32, name="part", tag="plane1_%d" % (2 * h + kb), align_bytes=64) for kb in range(KB)
            ]
            for kb in range(KB):
                nc.vector.tensor_tensor(parts[kb][:], dx[kb][:].indirect(pos1_sb[:, lists]), ds[kb, h][:], ADD)
            for kb in range(KB):
                res = held.tile([P, W], F32, name="res", tag="plane2_%d" % (2 * h + kb), align_bytes=64)
                cuts = (0, W - quarter, W) if (h, kb) == (HALVES - 1, KB - 1) else (0, W)
                for c0, c1 in zip(cuts, cuts[1:]):
                    t0, t1 = h * W + c0, h * W + c1
                    nc.vector.tensor_tensor(
                        res[:, c0:c1], dx[kb][:].indirect(pos2_sb[:, t0 // 16:t1 // 16]), parts[kb][:, c0:c1], ADD
                    )
                    queue = nc.scalar if (kb, t1) == (KB - 1, T) else nc.sync
                    queue.dma_start(out=out[kb * P:(kb + 1) * P, t0:t1], in_=res[:, c0:c1])
